import numpy as np
import ml_dtypes


def mxq(x, axis, fmt="e4m3"):
    dtype, down = {"e4m3": (ml_dtypes.float8_e4m3fn, 7), "e5m2": (ml_dtypes.float8_e5m2, 14)}[fmt]
    v = np.moveaxis(np.asarray(x, np.float32).astype(ml_dtypes.bfloat16).astype(np.float64), axis, -1)
    blocks = v.reshape(v.shape[:-1] + (-1, 32))
    amax = np.abs(blocks).max(-1, keepdims=True)
    byte = np.maximum(np.where(amax > 0, np.frexp(amax)[1] - 1 + 127, 0) - down, 1)
    scale = np.exp2(byte - 127.0)
    codes = (blocks / scale).astype(np.float32).astype(dtype).astype(np.float64)
    return np.moveaxis((codes * scale).reshape(v.shape), -1, axis)


WIDE = False


def mx_kscale(k):
    if not WIDE:
        return np.ones(k)
    levels = np.array([10, -10, 5, -5, 0])
    if k % 512:
        return np.exp2(np.random.permutation(np.resize(levels, k // 32))).repeat(32)
    a = np.empty((k // 512, 16))
    for p in range(k // 512):
        a[p, :8] = np.random.permutation(np.resize(levels, 8))
        for g in range(8):
            far = levels[np.abs(levels - a[p, g]) >= 10]
            a[p, g + 8] = far[np.random.randint(len(far))]
    return np.exp2(a.ravel()).repeat(32)


BF16 = ml_dtypes.bfloat16


def bf(x):
    return np.asarray(x, np.float32).astype(BF16)


def f64(x):
    return np.asarray(x).astype(np.float64)


E2M1 = np.array([0.0, 0.5, 1.0, 1.5, 2.0, 3.0, 4.0, 6.0, -0.0, -0.5, -1.0, -1.5, -2.0, -3.0, -4.0, -6.0])


def pack_weight(w, fmt):
    k, n = w.shape
    w = f64(bf(w)).reshape(k // 32, 32, n)
    amax = np.abs(w).max(1)
    if fmt == "e4m3":
        byte = np.frexp(amax)[1] - 1 + 127 - 7
    else:
        mant, ex = np.frexp(amax / 6.0)
        byte = np.where(mant > 0.5, ex, ex - 1) + 127
    byte = np.clip(np.where(amax > 0, byte, 1), 1, 254)
    scaled = (w * np.exp2(127.0 - byte)[:, None, :]).reshape(k, n).astype(np.float32)
    by_word = np.ascontiguousarray(scaled.reshape(k // 512, 128, 4, n).transpose(0, 1, 3, 2))
    if fmt == "e4m3":
        words = by_word.astype(ml_dtypes.float8_e4m3fn).view(np.uint8)
    else:
        c = by_word.astype(ml_dtypes.float4_e2m1fn).view(np.uint8) & 0xF
        words = c[..., 0::2] | (c[..., 1::2] << 4)
    return np.ascontiguousarray(words), np.ascontiguousarray(byte.astype(np.uint8).reshape(k // 512, 16, n))


def unpack_weight(words, scales, fmt):
    g, p, n, _ = words.shape
    if fmt == "e4m3":
        vals = np.ascontiguousarray(words).view(ml_dtypes.float8_e4m3fn).astype(np.float64)
    else:
        nib = np.empty((g, p, n, 4), np.uint8)
        nib[..., 0::2] = words & 0xF
        nib[..., 1::2] = words >> 4
        vals = E2M1[nib]
    vals = vals * np.repeat(np.exp2(scales.astype(np.float64) - 127.0), 8, axis=1)[..., None]
    return vals.transpose(0, 1, 3, 2).reshape(g * 512, n)
def pack4(w):
    words, scales = pack_weight(w, "e2m1")
    return words.reshape(words.shape[0], 128, -1), scales


def unpack4(words, scales):
    return unpack_weight(words.reshape(words.shape[0], 128, -1, 2), scales, "e2m1")


M, K, N = 1024, 1536, 1024


def setup_inputs():
    s = mx_kscale(K)
    win = np.abs(np.random.standard_normal((M, K))) / np.sqrt(K)
    spread = 0.5 + np.random.random(N)
    energy = np.square(np.random.standard_normal((K, N))) * spread / np.sqrt(K)
    cross = np.random.standard_normal((K, N))
    target = np.random.standard_normal((K, N))
    e_words, e_scales = pack4(energy / s[:, None])
    c_words, c_scales = pack_weight(cross / s[:, None], "e4m3")
    return {"win": bf(win * s),
            "e_words": e_words, "e_scales": e_scales,
            "c_words": c_words, "c_scales": c_scales,
            "target": bf(target / s[:, None]),
            "guide": bf(np.random.standard_normal((M, N))),
            "reg": bf(0.2 + 0.1 * np.abs(np.random.standard_normal(N)))}


def reference(win, e_words, e_scales, c_words, c_scales, target, guide, reg):
    b = mxq(f64(win), 1, "e4m3")
    var = b @ unpack4(e_words, e_scales)
    cov = b @ unpack_weight(c_words, c_scales, "e4m3")
    mean = b @ mxq(f64(target), 0, "e4m3")
    slope = cov / (var + f64(reg))
    return slope * f64(guide) + mean

@@ -1,0 +1,284 @@
+from contextlib import ExitStack
+
+import concourse.mybir as mybir
+from concourse.masks import make_identity
+
+M, K, N = 1024, 1536, 1024
+FLOPS = 3 * 2 * M * K * N
+
+F32 = mybir.dt.float32
+BF16 = mybir.dt.bfloat16
+I32 = mybir.dt.int32
+U32 = mybir.dt.uint32
+U8 = mybir.dt.uint8
+FP8X4 = mybir.dt.float8_e4m3fn_x4
+FP4X4 = mybir.dt.float4_e2m1fn_x4
+ACT = mybir.ActivationFunctionType
+ALU = mybir.AluOpType
+
+P = 128
+PACK = 4
+K_PASS = P * PACK
+PASSES = K // K_PASS
+TILES = M // P
+HALF = 512
+HALVES = N // HALF
+UNITS = TILES * HALVES
+BANKS = 8
+RUN_BANKS = 3
+GAIN_BUFS = 4
+
+
+def tile_guided_filter_windows_s10_kernel(tc, win, e_words, e_scales, c_words, c_scales, target, guide, reg, out):
+    nc = tc.nc
+    with ExitStack() as ctx:
+        keep = ctx.enter_context(tc.tile_pool(name="keep", bufs=1))
+        work = ctx.enter_context(tc.tile_pool(name="work", bufs=1))
+        psum = ctx.enter_context(tc.psum_pool(name="psum", bufs=1))
+        ctx.enter_context(tc.manual_schedule())
+
+        def kept(name, shape, dtype):
+            return keep.tile(shape, dtype, name=name, align_bytes=64)
+
+        free_banks = list(range(BANKS))
+
+        def take_bank():
+            index = free_banks.pop(0)
+            return index, psum.tile([P, HALF], F32, name="bank%d" % index)
+
+        e_plane = kept("e_plane", [P, PASSES, N], U8)
+        c_plane = kept("c_plane", [P, PASSES, N], U8)
+        nc.vector.memset(e_plane[:].bitcast(I32), 0)
+        nc.vector.memset(c_plane[:].bitcast(I32), 0)
+        identity = kept("identity", [P, P], F32)
+        make_identity(nc, identity[:])
+        warm_in = kept("warm_in", [P, 8], F32)
+        warm_out = kept("warm_out", [P, 8], F32)
+        nc.gpsimd.memset(warm_in[:], 1.0)
+        nc.scalar.activation(out=warm_out[:], in_=warm_in[:], func=ACT.Abs_reciprocal_sqrt)
+
+        win_words = {}
+
+        def load_win(first, count):
+            raw = kept("win_raw%d" % first, [P, count, K], BF16)
+            nc.sync.dma_start(out=raw[:], in_=win[first * P : (first + count) * P, :].rearrange("(t p) k -> p t k", p=P))
+            for t in range(count):
+                win_words[first + t] = raw[:, t, :].bitcast(F32)
+
+        def load_plane(plane, scales):
+            rows = scales.rearrange("g r n -> r g n")
+            for q in range(4):
+                nc.sync.dma_start(out=plane[32 * q : 32 * q + 4, :, :].bitcast(I32), in_=rows[4 * q : 4 * q + 4, :, :].bitcast(I32))
+
+        def load_words(name, words, width):
+            codes = kept(name, [P, PASSES, width], U8)
+            nc.sync.dma_start(out=codes[:].bitcast(I32), in_=words.bitcast(I32))
+            return codes
+
+        def load_target(g):
+            raw = kept("target_raw%d" % g, [P, PACK, N], BF16)
+            nc.sync.dma_start(out=raw[:], in_=target[g * K_PASS : (g + 1) * K_PASS, :].rearrange("(p j) n -> p j n", j=PACK))
+            return raw
+
+        guide_rows = {}
+
+        def load_guide(first):
+            raw = kept("guide%d" % first, [P, 2, N], BF16)
+            nc.sync.dma_start(out=raw[:], in_=guide[first * P : (first + 2) * P, :].rearrange("(t p) n -> p t n", p=P))
+            for t in range(2):
+                guide_rows[first + t] = raw[:, t, :]
+
+        e_rows = e_words.rearrange("g p b -> p g b")
+        c_rows = c_words.rearrange("g p n t -> p g (n t)")
+        load_win(0, 1)
+        reg_rows = kept("reg_rows", [P, N // P], BF16)
+        nc.sync.dma_start(out=reg_rows[:], in_=reg.rearrange("(p c) -> p c", p=P))
+        load_win(1, 1)
+        load_plane(e_plane, e_scales)
+        e_codes = [load_words("e_codes%d" % h, e_rows[:, :, 2 * HALF * h : 2 * HALF * (h + 1)], 2 * HALF) for h in range(HALVES)]
+        target_raw = []
+        for g in range(PASSES):
+            load_win(2 + 2 * g, 2)
+            target_raw.append(load_target(g))
+        load_plane(c_plane, c_scales)
+        c_codes = [load_words("c_codes0", c_rows[:, :, 0 : 4 * HALF], 4 * HALF)]
+        for first in range(0, TILES, 2):
+            load_guide(first)
+        c_codes.append(load_words("c_codes1", c_rows[:, :, 4 * HALF : 8 * HALF], 4 * HALF))
+
+        win_grouped = {}
+        win_mx = {}
+
+        def turn_windows(run):
+            held = []
+            for b in range(RUN_BANKS * run, RUN_BANKS * (run + 1)):
+                index, bank = take_bank()
+                for s in range(2):
+                    tile, g = divmod(2 * b + s, PASSES)
+                    for u in range(2):
+                        col = (2 * s + u) * P
+                        nc.tensor.transpose(bank[:, col : col + P], win_words[tile][:, 2 * P * g + u : 2 * P * (g + 1) : 2], identity[:])
+                held.append((b, index, bank))
+            for b, index, bank in held:
+                grouped = work.tile([P, 2 * K_PASS], BF16, name="win_grouped", bufs=RUN_BANKS, align_bytes=64)
+                nc.scalar.copy(
+                    out=grouped[:].bitcast(F32).rearrange("p (s m u) -> p s m u", s=2, u=2),
+                    in_=bank[:].rearrange("p (s u m) -> p s m u", s=2, u=2),
+                )
+                free_banks.append(index)
+                win_grouped[b] = grouped
+
+        def quantize_windows(run):
+            for b in range(RUN_BANKS * run, RUN_BANKS * (run + 1)):
+                codes = kept("win_codes%d" % b, [P, 2 * P], U32)
+                plane = kept("win_plane%d" % b, [P, 2 * P], U8)
+                nc.vector.quantize_mx(out=codes[:].bitcast(FP8X4), scales=plane[:], in_=win_grouped[b][:])
+                for s in range(2):
+                    win_mx[divmod(2 * b + s, PASSES)] = (codes[:, s * P : (s + 1) * P], plane[:, s * P : (s + 1) * P])
+
+        def product(tile, operands):
+            index, bank = take_bank()
+            for g in range(PASSES):
+                codes, plane = win_mx[(tile, g)]
+                rhs, rhs_scale = operands[g]
+                nc.tensor.matmul_mx(
+                    out=bank[:], lhsT=codes.bitcast(FP8X4), lhsT_scale=plane, rhs=rhs, rhs_scale=rhs_scale,
+                    start=(g == 0), stop=(g == PASSES - 1),
+                )
+            return index, bank
+
+        def cols(h):
+            return slice(h * HALF, (h + 1) * HALF)
+
+        e_operands = [[(e_codes[h][:, g, :].bitcast(FP4X4), e_plane[:, g, cols(h)]) for g in range(PASSES)] for h in range(HALVES)]
+        c_operands = [[(c_codes[h][:, g, :].bitcast(FP8X4), c_plane[:, g, cols(h)]) for g in range(PASSES)] for h in range(HALVES)]
+        t_operands = [[None] * PASSES for h in range(HALVES)]
+        target_grouped = {}
+
+        def interleave_target(g, h):
+            grouped = work.tile([P, HALF, PACK], BF16, name="target_grouped%d" % h, bufs=(2 if h == 0 else PASSES), align_bytes=64)
+            dst = grouped[:].rearrange("p (c i) j -> p c j i", i=4)
+            src = target_raw[g][:, :, cols(h)].rearrange("p j (c i) -> p c j i", i=4)
+            if h == 0:
+                nc.vector.tensor_copy(out=dst, in_=src)
+            else:
+                nc.scalar.copy(out=dst, in_=src)
+            target_grouped[(g, h)] = grouped
+
+        def quantize_target(g, h):
+            codes = kept("target_codes%d_%d" % (g, h), [P, HALF], U32)
+            plane = kept("target_plane%d_%d" % (g, h), [P, HALF], U8)
+            nc.vector.quantize_mx(out=codes[:].bitcast(FP8X4), scales=plane[:], in_=target_grouped[(g, h)][:].rearrange("p n j -> p (n j)"))
+            t_operands[h][g] = (codes[:].bitcast(FP8X4), plane[:])
+
+        reg_all = kept("reg_all", [P, N], BF16)
+
+        def spread_reg():
+            index, bank = take_bank()
+            words = reg_rows[:].bitcast(F32)
+            for c in range(4):
+                nc.tensor.transpose(bank[:, c * P : (c + 1) * P], words[:, c : c + 1].to_broadcast([P, P]), identity[:])
+            nc.vector.tensor_copy(
+                out=reg_all[:].bitcast(F32).rearrange("q (p c) -> q p c", c=4),
+                in_=bank[:].rearrange("q (c p) -> q p c", c=4),
+            )
+            free_banks.append(index)
+
+        variance = {}
+        divisor = {}
+
+        def multiply_energy(s):
+            tile, h = divmod(s, HALVES)
+            variance[s] = product(tile, e_operands[h])
+
+        def add_reg(s):
+            tile, h = divmod(s, HALVES)
+            index, bank = variance[s]
+            d = kept("divisor%d" % s, [P, HALF], F32)
+            nc.vector.tensor_tensor(out=d[:], in0=bank[:], in1=reg_all[:, cols(h)], op=ALU.add)
+            free_banks.append(index)
+            divisor[(h, tile)] = d
+
+        order = [(h, tile) for h in range(HALVES) for tile in range(TILES)]
+        roots = {}
+
+        def inverse_root(i):
+            root = work.tile([P, HALF], F32, name="root", bufs=3)
+            nc.scalar.activation(out=root[:], in_=divisor[order[i]][:], func=ACT.Abs_reciprocal_sqrt)
+            roots[i] = root
+
+        def square_root_back(i):
+            nc.scalar.activation(out=divisor[order[i]][:], in_=roots[i][:], func=ACT.Square)
+
+        gains = {}
+
+        def make_gain(i):
+            h, tile = order[i]
+            gain = work.tile([P, HALF], F32, name="gain", bufs=GAIN_BUFS)
+            nc.gpsimd.tensor_tensor(out=gain[:], in0=divisor[order[i]][:], in1=guide_rows[tile][:, cols(h)], op=ALU.mult)
+            gains[i] = gain
+
+        turn_windows(0)
+        quantize_windows(0)
+        spread_reg()
+        multiply_energy(0)
+        add_reg(0)
+        inverse_root(0)
+        square_root_back(0)
+        multiply_energy(1)
+        add_reg(1)
+        for g in range(PASSES):
+            s = 4 * g + 2
+            turn_windows(g + 1)
+            multiply_energy(s)
+            quantize_windows(g + 1)
+            add_reg(s)
+            interleave_target(g, 0)
+            interleave_target(g, 1)
+            if g + 1 < PASSES:
+                inverse_root(g + 1)
+                square_root_back(g + 1)
+            multiply_energy(s + 1)
+            add_reg(s + 1)
+            quantize_target(g, 0)
+            for later in range(s + 2, s + 4):
+                multiply_energy(later)
+                add_reg(later)
+        for s in range(4 * PASSES + 2, UNITS):
+            multiply_energy(s)
+            add_reg(s)
+        inverse_root(PASSES)
+        for i in range(PASSES, UNITS):
+            if i + 1 < UNITS:
+                inverse_root(i + 1)
+            square_root_back(i)
+
+        slopes = {}
+
+        def multiply_cross(i):
+            h, tile = order[i]
+            index, bank = product(tile, c_operands[h])
+            part = work.tile([P, HALF], F32, name="part", bufs=3)
+            nc.vector.tensor_tensor(out=part[:], in0=bank[:], in1=gains[i][:], op=ALU.mult)
+            free_banks.append(index)
+            slopes[i] = part
+            if i + GAIN_BUFS < UNITS:
+                make_gain(i + GAIN_BUFS)
+
+        def multiply_target(i):
+            h, tile = order[i]
+            index, bank = product(tile, t_operands[h])
+            result = work.tile([P, HALF], F32, name="result", bufs=4)
+            nc.vector.tensor_tensor(out=result[:], in0=bank[:], in1=slopes[i][:], op=ALU.add)
+            free_banks.append(index)
+            nc.sync.dma_start(out=out[tile * P : (tile + 1) * P, cols(h)], in_=result[:])
+
+        for i in range(GAIN_BUFS):
+            make_gain(i)
+        multiply_cross(0)
+        for i in range(UNITS):
+            if i + 1 < UNITS:
+                multiply_cross(i + 1)
+            multiply_target(i)
+            if i % 2 == 1 and i // 2 < PASSES:
+                quantize_target(i // 2, 1)

@@ -46,16 +46,19 @@ def tile_guided_filter_windows_s10_kernel(tc, win, e_words, e_scales, c_words, c
             index = free_banks.pop(0)
             return index, psum.tile([P, HALF], F32, name="bank%d" % index)
 
-        e_plane = kept("e_plane", [P, PASSES, N], U8)
+        e_planes = [kept("e_plane%d" % h, [P, PASSES, HALF], U8) for h in range(HALVES)]
         c_plane = kept("c_plane", [P, PASSES, N], U8)
-        nc.vector.memset(e_plane[:].bitcast(I32), 0)
-        nc.vector.memset(c_plane[:].bitcast(I32), 0)
+        warm_values = kept("warm_values", [P, K_PASS], BF16)
+        warm_codes = kept("warm_codes", [P, P], U32)
+        warm_plane = kept("warm_plane", [P, P], U8)
+        nc.gpsimd.memset(warm_values[:].bitcast(I32), 0x3F803F80)
+        nc.vector.quantize_mx(out=warm_codes[:].bitcast(FP8X4), scales=warm_plane[:], in_=warm_values[:])
+        for plane in e_planes + [c_plane]:
+            nc.vector.memset(plane[:].bitcast(I32), 0)
         identity = kept("identity", [P, P], F32)
         make_identity(nc, identity[:])
-        warm_in = kept("warm_in", [P, 8], F32)
         warm_out = kept("warm_out", [P, 8], F32)
-        nc.gpsimd.memset(warm_in[:], 1.0)
-        nc.scalar.activation(out=warm_out[:], in_=warm_in[:], func=ACT.Abs_reciprocal_sqrt)
+        nc.scalar.activation(out=warm_out[:], in_=warm_values[:, 0:8], func=ACT.Abs_reciprocal_sqrt)
 
         win_words = {}
 
@@ -65,20 +68,25 @@ def tile_guided_filter_windows_s10_kernel(tc, win, e_words, e_scales, c_words, c
             for t in range(count):
                 win_words[first + t] = raw[:, t, :].bitcast(F32)
 
-        def load_plane(plane, scales):
+        def cols(h):
+            return slice(h * HALF, (h + 1) * HALF)
+
+        def load_plane(plane, scales, columns):
             rows = scales.rearrange("g r n -> r g n")
             for q in range(4):
-                nc.sync.dma_start(out=plane[32 * q : 32 * q + 4, :, :].bitcast(I32), in_=rows[4 * q : 4 * q + 4, :, :].bitcast(I32))
+                nc.sync.dma_start(out=plane[32 * q : 32 * q + 4, :, :].bitcast(I32), in_=rows[4 * q : 4 * q + 4, :, columns].bitcast(I32))
 
         def load_words(name, words, width):
             codes = kept(name, [P, PASSES, width], U8)
             nc.sync.dma_start(out=codes[:].bitcast(I32), in_=words.bitcast(I32))
             return codes
 
-        def load_target(g):
-            raw = kept("target_raw%d" % g, [P, PACK, N], BF16)
-            nc.sync.dma_start(out=raw[:], in_=target[g * K_PASS : (g + 1) * K_PASS, :].rearrange("(p j) n -> p j n", j=PACK))
-            return raw
+        target_raw = {}
+
+        def load_target(g, h):
+            raw = kept("target_raw%d_%d" % (g, h), [P, PACK, HALF], BF16)
+            nc.sync.dma_start(out=raw[:], in_=target[g * K_PASS : (g + 1) * K_PASS, cols(h)].rearrange("(p j) n -> p j n", j=PACK))
+            target_raw[(g, h)] = raw
 
         guide_rows = {}
 
@@ -93,77 +101,79 @@ def tile_guided_filter_windows_s10_kernel(tc, win, e_words, e_scales, c_words, c
         load_win(0, 1)
         reg_rows = kept("reg_rows", [P, N // P], BF16)
         nc.sync.dma_start(out=reg_rows[:], in_=reg.rearrange("(p c) -> p c", p=P))
+        load_plane(e_planes[0], e_scales, cols(0))
+        e_codes = [load_words("e_codes0", e_rows[:, :, 0 : 2 * HALF], 2 * HALF)]
         load_win(1, 1)
-        load_plane(e_plane, e_scales)
-        e_codes = [load_words("e_codes%d" % h, e_rows[:, :, 2 * HALF * h : 2 * HALF * (h + 1)], 2 * HALF) for h in range(HALVES)]
-        target_raw = []
-        for g in range(PASSES):
-            load_win(2 + 2 * g, 2)
-            target_raw.append(load_target(g))
-        load_plane(c_plane, c_scales)
-        c_codes = [load_words("c_codes0", c_rows[:, :, 0 : 4 * HALF], 4 * HALF)]
+        load_plane(e_planes[1], e_scales, cols(1))
+        e_codes.append(load_words("e_codes1", e_rows[:, :, 2 * HALF : 4 * HALF], 2 * HALF))
+        chunks = [(g, h) for h in range(HALVES) for g in range(PASSES)]
+        for n, (g, h) in enumerate(chunks):
+            load_win(2 + n, 1)
+            load_target(g, h)
+        load_plane(c_plane, c_scales, slice(0, N))
+        c_codes = [load_words("c_codes%d" % h, c_rows[:, :, 4 * HALF * h : 4 * HALF * (h + 1)], 4 * HALF) for h in range(HALVES)]
         for first in range(0, TILES, 2):
             load_guide(first)
-        c_codes.append(load_words("c_codes1", c_rows[:, :, 4 * HALF : 8 * HALF], 4 * HALF))
 
-        win_grouped = {}
+        win_grouped = []
         win_mx = {}
 
-        def turn_windows(run):
+        def turn_windows(tiles, per_bank):
+            slabs = [(tile, g) for tile in tiles for g in range(PASSES)]
             held = []
-            for b in range(RUN_BANKS * run, RUN_BANKS * (run + 1)):
+            for first in range(0, len(slabs), per_bank):
                 index, bank = take_bank()
-                for s in range(2):
-                    tile, g = divmod(2 * b + s, PASSES)
+                together = slabs[first : first + per_bank]
+                for s, (tile, g) in enumerate(together):
                     for u in range(2):
                         col = (2 * s + u) * P
                         nc.tensor.transpose(bank[:, col : col + P], win_words[tile][:, 2 * P * g + u : 2 * P * (g + 1) : 2], identity[:])
-                held.append((b, index, bank))
-            for b, index, bank in held:
-                grouped = work.tile([P, 2 * K_PASS], BF16, name="win_grouped", bufs=RUN_BANKS, align_bytes=64)
+                held.append((together, index, bank))
+            for together, index, bank in held:
+                count = len(together)
+                grouped = work.tile([P, count * K_PASS], BF16, name="win_grouped", bufs=RUN_BANKS, align_bytes=64)
                 nc.scalar.copy(
-                    out=grouped[:].bitcast(F32).rearrange("p (s m u) -> p s m u", s=2, u=2),
-                    in_=bank[:].rearrange("p (s u m) -> p s m u", s=2, u=2),
+                    out=grouped[:].bitcast(F32).rearrange("p (s m u) -> p s m u", s=count, u=2),
+                    in_=bank[:, 0 : count * 2 * P].rearrange("p (s u m) -> p s m u", s=count, u=2),
                 )
                 free_banks.append(index)
-                win_grouped[b] = grouped
+                win_grouped.append((together, grouped))
 
-        def quantize_windows(run):
-            for b in range(RUN_BANKS * run, RUN_BANKS * (run + 1)):
-                codes = kept("win_codes%d" % b, [P, 2 * P], U32)
-                plane = kept("win_plane%d" % b, [P, 2 * P], U8)
-                nc.vector.quantize_mx(out=codes[:].bitcast(FP8X4), scales=plane[:], in_=win_grouped[b][:])
-                for s in range(2):
-                    win_mx[divmod(2 * b + s, PASSES)] = (codes[:, s * P : (s + 1) * P], plane[:, s * P : (s + 1) * P])
+        def quantize_windows():
+            for together, grouped in win_grouped:
+                count = len(together)
+                codes = kept("win_codes%d_%d" % together[0], [P, count * P], U32)
+                plane = kept("win_plane%d_%d" % together[0], [P, count * P], U8)
+                nc.vector.quantize_mx(out=codes[:].bitcast(FP8X4), scales=plane[:], in_=grouped[:])
+                for s, slab in enumerate(together):
+                    win_mx[slab] = (codes[:, s * P : (s + 1) * P], plane[:, s * P : (s + 1) * P])
+            win_grouped.clear()
 
-        def product(tile, operands):
+        def product(tile, operands, columns=slice(0, HALF)):
             index, bank = take_bank()
+            sums = bank[:, 0 : columns.stop - columns.start]
             for g in range(PASSES):
                 codes, plane = win_mx[(tile, g)]
                 rhs, rhs_scale = operands[g]
                 nc.tensor.matmul_mx(
-                    out=bank[:], lhsT=codes.bitcast(FP8X4), lhsT_scale=plane, rhs=rhs, rhs_scale=rhs_scale,
+                    out=sums, lhsT=codes.bitcast(FP8X4), lhsT_scale=plane, rhs=rhs[:, columns], rhs_scale=rhs_scale[:, columns],
                     start=(g == 0), stop=(g == PASSES - 1),
                 )
-            return index, bank
+            return index, sums
 
-        def cols(h):
-            return slice(h * HALF, (h + 1) * HALF)
-
-        e_operands = [[(e_codes[h][:, g, :].bitcast(FP4X4), e_plane[:, g, cols(h)]) for g in range(PASSES)] for h in range(HALVES)]
+        e_operands = [[(e_codes[h][:, g, :].bitcast(FP4X4), e_planes[h][:, g, :]) for g in range(PASSES)] for h in range(HALVES)]
         c_operands = [[(c_codes[h][:, g, :].bitcast(FP8X4), c_plane[:, g, cols(h)]) for g in range(PASSES)] for h in range(HALVES)]
         t_operands = [[None] * PASSES for h in range(HALVES)]
         target_grouped = {}
 
-        def interleave_target(g, h):
-            grouped = work.tile([P, HALF, PACK], BF16, name="target_grouped%d" % h, bufs=(2 if h == 0 else PASSES), align_bytes=64)
-            dst = grouped[:].rearrange("p (c i) j -> p c j i", i=4)
-            src = target_raw[g][:, :, cols(h)].rearrange("p j (c i) -> p c j i", i=4)
-            if h == 0:
-                nc.vector.tensor_copy(out=dst, in_=src)
-            else:
-                nc.scalar.copy(out=dst, in_=src)
-            target_grouped[(g, h)] = grouped
+        def interleave_target(g, h, part, copy):
+            if part == 0:
+                target_grouped[(g, h)] = work.tile([P, HALF, PACK], BF16, name="target_grouped", bufs=2, align_bytes=64)
+            columns = slice(part * HALF // 2, (part + 1) * HALF // 2)
+            copy(
+                out=target_grouped[(g, h)][:, columns, :].rearrange("p (c i) j -> p c j i", i=4),
+                in_=target_raw[(g, h)][:, :, columns].rearrange("p j (c i) -> p c j i", i=4),
+            )
 
         def quantize_target(g, h):
             codes = kept("target_codes%d_%d" % (g, h), [P, HALF], U32)
@@ -195,7 +205,7 @@ def tile_guided_filter_windows_s10_kernel(tc, win, e_words, e_scales, c_words, c
             tile, h = divmod(s, HALVES)
             index, bank = variance[s]
             d = kept("divisor%d" % s, [P, HALF], F32)
-            nc.vector.tensor_tensor(out=d[:], in0=bank[:], in1=reg_all[:, cols(h)], op=ALU.add)
+            nc.vector.tensor_tensor(out=d[:], in0=bank, in1=reg_all[:, cols(h)], op=ALU.add)
             free_banks.append(index)
             divisor[(h, tile)] = d
 
@@ -218,40 +228,62 @@ def tile_guided_filter_windows_s10_kernel(tc, win, e_words, e_scales, c_words, c
             nc.gpsimd.tensor_tensor(out=gain[:], in0=divisor[order[i]][:], in1=guide_rows[tile][:, cols(h)], op=ALU.mult)
             gains[i] = gain
 
-        turn_windows(0)
-        quantize_windows(0)
+        def energy_unit(s):
+            multiply_energy(s)
+            add_reg(s)
+
+        def reciprocals(first, last):
+            inverse_root(first)
+            for i in range(first, last):
+                if i + 1 < last:
+                    inverse_root(i + 1)
+                square_root_back(i)
+
+        def warm_tensor_engine(count):
+            index, bank = take_bank()
+            for step in range(count):
+                nc.tensor.matmul_mx(
+                    out=bank[:, 0:P], lhsT=warm_codes[:].bitcast(FP8X4), lhsT_scale=warm_plane[:],
+                    rhs=warm_codes[:].bitcast(FP8X4), rhs_scale=warm_plane[:], start=(step == 0), stop=(step == count - 1),
+                )
+            free_banks.append(index)
+
+        on_vector = nc.vector.tensor_copy
+        on_scalar = nc.scalar.copy
+        warm_tensor_engine(10)
+        turn_windows([0], 1)
+        quantize_windows()
         spread_reg()
-        multiply_energy(0)
-        add_reg(0)
-        inverse_root(0)
-        square_root_back(0)
-        multiply_energy(1)
-        add_reg(1)
-        for g in range(PASSES):
-            s = 4 * g + 2
-            turn_windows(g + 1)
-            multiply_energy(s)
-            quantize_windows(g + 1)
-            add_reg(s)
-            interleave_target(g, 0)
-            interleave_target(g, 1)
-            if g + 1 < PASSES:
-                inverse_root(g + 1)
-                square_root_back(g + 1)
-            multiply_energy(s + 1)
-            add_reg(s + 1)
-            quantize_target(g, 0)
-            for later in range(s + 2, s + 4):
-                multiply_energy(later)
-                add_reg(later)
-        for s in range(4 * PASSES + 2, UNITS):
-            multiply_energy(s)
-            add_reg(s)
-        inverse_root(PASSES)
-        for i in range(PASSES, UNITS):
-            if i + 1 < UNITS:
-                inverse_root(i + 1)
-            square_root_back(i)
+        energy_unit(0)
+        turn_windows([1], 2)
+        quantize_windows()
+        reciprocals(0, 1)
+        energy_unit(1)
+
+        for tile in range(2, TILES):
+            n = tile - 3
+            turn_windows([tile], 2)
+            if n >= 1:
+                quantize_target(*chunks[n - 1])
+            if n >= 0:
+                interleave_target(*chunks[n], 0, on_vector)
+                interleave_target(*chunks[n], 1, on_scalar)
+            if n >= 1:
+                if n % 2 == 1:
+                    inverse_root((n + 1) // 2)
+                else:
+                    square_root_back(n // 2)
+            multiply_energy(2 * tile - 2)
+            quantize_windows()
+            add_reg(2 * tile - 2)
+            energy_unit(2 * tile - 1)
+        quantize_target(*chunks[4])
+        energy_unit(14)
+        energy_unit(15)
+        reciprocals(3, 8)
+        interleave_target(*chunks[5], 0, on_scalar)
+        interleave_target(*chunks[5], 1, on_scalar)
+        reciprocals(8, UNITS)
 
         slopes = {}
 
@@ -259,19 +291,19 @@ def tile_guided_filter_windows_s10_kernel(tc, win, e_words, e_scales, c_words, c
             h, tile = order[i]
             index, bank = product(tile, c_operands[h])
             part = work.tile([P, HALF], F32, name="part", bufs=3)
-            nc.vector.tensor_tensor(out=part[:], in0=bank[:], in1=gains[i][:], op=ALU.mult)
+            nc.vector.tensor_tensor(out=part[:], in0=bank, in1=gains[i][:], op=ALU.mult)
             free_banks.append(index)
             slopes[i] = part
             if i + GAIN_BUFS < UNITS:
                 make_gain(i + GAIN_BUFS)
 
-        def multiply_target(i):
+        def multiply_target(i, columns):
             h, tile = order[i]
-            index, bank = product(tile, t_operands[h])
-            result = work.tile([P, HALF], F32, name="result", bufs=4)
-            nc.vector.tensor_tensor(out=result[:], in0=bank[:], in1=slopes[i][:], op=ALU.add)
+            index, bank = product(tile, t_operands[h], columns)
+            result = work.tile([P, columns.stop - columns.start], F32, name="result", bufs=4)
+            nc.vector.tensor_tensor(out=result[:], in0=bank, in1=slopes[i][:, columns], op=ALU.add)
             free_banks.append(index)
-            nc.sync.dma_start(out=out[tile * P : (tile + 1) * P, cols(h)], in_=result[:])
+            nc.sync.dma_start(out=out[tile * P : (tile + 1) * P, cols(h)][:, columns], in_=result[:])
 
         for i in range(GAIN_BUFS):
             make_gain(i)
@@ -279,6 +311,9 @@ def tile_guided_filter_windows_s10_kernel(tc, win, e_words, e_scales, c_words, c
         for i in range(UNITS):
             if i + 1 < UNITS:
                 multiply_cross(i + 1)
-            multiply_target(i)
-            if i % 2 == 1 and i // 2 < PASSES:
-                quantize_target(i // 2, 1)
+                multiply_target(i, slice(0, HALF))
+            else:
+                for columns in (slice(0, 256), slice(256, 384), slice(384, 512)):
+                    multiply_target(i, columns)
+            if i == 4:
+                quantize_target(2, 1)

@@ -72,9 +72,9 @@ def tile_guided_filter_windows_s10_kernel(tc, win, e_words, e_scales, c_words, c
             return slice(h * HALF, (h + 1) * HALF)
 
         def load_plane(plane, scales, columns):
-            rows = scales.rearrange("g r n -> r g n")
-            for q in range(4):
-                nc.sync.dma_start(out=plane[32 * q : 32 * q + 4, :, :].bitcast(I32), in_=rows[4 * q : 4 * q + 4, :, columns].bitcast(I32))
+            rows = scales.rearrange("g (q r) n -> r q g n", r=4)
+            for r in range(4):
+                nc.sync.dma_start(out=plane[r:P:32, :, :].bitcast(I32), in_=rows[r, :, :, columns].bitcast(I32))
 
         def load_words(name, words, width):
             codes = kept(name, [P, PASSES, width], U8)
@@ -101,22 +101,48 @@ def tile_guided_filter_windows_s10_kernel(tc, win, e_words, e_scales, c_words, c
         load_win(0, 1)
         reg_rows = kept("reg_rows", [P, N // P], BF16)
         nc.sync.dma_start(out=reg_rows[:], in_=reg.rearrange("(p c) -> p c", p=P))
+        load_win(1, 1)
         load_plane(e_planes[0], e_scales, cols(0))
         e_codes = [load_words("e_codes0", e_rows[:, :, 0 : 2 * HALF], 2 * HALF)]
-        load_win(1, 1)
+        load_win(2, 1)
+        load_win(3, 1)
         load_plane(e_planes[1], e_scales, cols(1))
         e_codes.append(load_words("e_codes1", e_rows[:, :, 2 * HALF : 4 * HALF], 2 * HALF))
-        chunks = [(g, h) for h in range(HALVES) for g in range(PASSES)]
-        for n, (g, h) in enumerate(chunks):
-            load_win(2 + n, 1)
-            load_target(g, h)
+        load_target(0, 0)
+        load_win(4, 1)
+        load_win(5, 1)
+        load_target(1, 0)
+        load_win(6, 1)
+        load_win(7, 1)
+        load_target(2, 0)
+        load_target(0, 1)
         load_plane(c_plane, c_scales, slice(0, N))
-        c_codes = [load_words("c_codes%d" % h, c_rows[:, :, 4 * HALF * h : 4 * HALF * (h + 1)], 4 * HALF) for h in range(HALVES)]
-        for first in range(0, TILES, 2):
-            load_guide(first)
+        c_codes = [load_words("c_codes0", c_rows[:, :, 0 : 4 * HALF], 4 * HALF)]
+        load_guide(0)
+        load_target(1, 1)
+        load_guide(2)
+        load_target(2, 1)
+        load_guide(4)
+        load_guide(6)
+        c_codes.append(load_words("c_codes1", c_rows[:, :, 4 * HALF : 8 * HALF], 4 * HALF))
 
         win_grouped = []
         win_mx = {}
+
+        sorted_words = {}
+
+        def sort_words(tile, copy):
+            ordered = work.tile([P, K // 2], F32, name="win_sorted", bufs=2, align_bytes=64)
+            copy(
+                out=ordered[:].rearrange("m (g u c i) -> m g c u i", g=PASSES, u=2, i=4),
+                in_=win_words[tile].rearrange("m (g c i u) -> m g c u i", g=PASSES, u=2, i=4),
+            )
+            sorted_words[tile] = ordered
+
+        def words_of(tile, g, u):
+            if tile in sorted_words:
+                return sorted_words[tile][:, (2 * g + u) * P : (2 * g + u + 1) * P]
+            return win_words[tile][:, 2 * P * g + u : 2 * P * (g + 1) : 2]
 
         def turn_windows(tiles, per_bank):
             slabs = [(tile, g) for tile in tiles for g in range(PASSES)]
@@ -127,7 +153,7 @@ def tile_guided_filter_windows_s10_kernel(tc, win, e_words, e_scales, c_words, c
                 for s, (tile, g) in enumerate(together):
                     for u in range(2):
                         col = (2 * s + u) * P
-                        nc.tensor.transpose(bank[:, col : col + P], win_words[tile][:, 2 * P * g + u : 2 * P * (g + 1) : 2], identity[:])
+                        nc.tensor.transpose(bank[:, col : col + P], words_of(tile, g, u), identity[:])
                 held.append((together, index, bank))
             for together, index, bank in held:
                 count = len(together)
@@ -167,8 +193,8 @@ def tile_guided_filter_windows_s10_kernel(tc, win, e_words, e_scales, c_words, c
         target_grouped = {}
 
         def interleave_target(g, h, part, copy):
-            if part == 0:
-                target_grouped[(g, h)] = work.tile([P, HALF, PACK], BF16, name="target_grouped", bufs=2, align_bytes=64)
+            if (g, h) not in target_grouped:
+                target_grouped[(g, h)] = work.tile([P, HALF, PACK], BF16, name="target_grouped", bufs=3, align_bytes=64)
             columns = slice(part * HALF // 2, (part + 1) * HALF // 2)
             copy(
                 out=target_grouped[(g, h)][:, columns, :].rearrange("p (c i) j -> p c j i", i=4),
@@ -197,12 +223,14 @@ def tile_guided_filter_windows_s10_kernel(tc, win, e_words, e_scales, c_words, c
         variance = {}
         divisor = {}
 
+        energy_order = [(0, 0), (1, 0), (0, 1), (1, 1)] + [divmod(s, HALVES) for s in range(4, UNITS)]
+
         def multiply_energy(s):
-            tile, h = divmod(s, HALVES)
+            tile, h = energy_order[s]
             variance[s] = product(tile, e_operands[h])
 
         def add_reg(s):
-            tile, h = divmod(s, HALVES)
+            tile, h = energy_order[s]
             index, bank = variance[s]
             d = kept("divisor%d" % s, [P, HALF], F32)
             nc.vector.tensor_tensor(out=d[:], in0=bank, in1=reg_all[:, cols(h)], op=ALU.add)
@@ -250,40 +278,65 @@ def tile_guided_filter_windows_s10_kernel(tc, win, e_words, e_scales, c_words, c
 
         on_vector = nc.vector.tensor_copy
         on_scalar = nc.scalar.copy
-        warm_tensor_engine(10)
-        turn_windows([0], 1)
+        warm_tensor_engine(12)
+        def interleave_whole(g, h, copy):
+            for part in range(2):
+                interleave_target(g, h, part, copy)
+
+        turn_windows([0, 1], 2)
         quantize_windows()
         spread_reg()
         energy_unit(0)
-        turn_windows([1], 2)
-        quantize_windows()
-        reciprocals(0, 1)
+        sort_words(2, on_scalar)
         energy_unit(1)
 
-        for tile in range(2, TILES):
-            n = tile - 3
-            turn_windows([tile], 2)
-            if n >= 1:
-                quantize_target(*chunks[n - 1])
-            if n >= 0:
-                interleave_target(*chunks[n], 0, on_vector)
-                interleave_target(*chunks[n], 1, on_scalar)
-            if n >= 1:
-                if n % 2 == 1:
-                    inverse_root((n + 1) // 2)
-                else:
-                    square_root_back(n // 2)
-            multiply_energy(2 * tile - 2)
-            quantize_windows()
-            add_reg(2 * tile - 2)
-            energy_unit(2 * tile - 1)
-        quantize_target(*chunks[4])
-        energy_unit(14)
-        energy_unit(15)
-        reciprocals(3, 8)
-        interleave_target(*chunks[5], 0, on_scalar)
-        interleave_target(*chunks[5], 1, on_scalar)
-        reciprocals(8, UNITS)
+        turn_windows([2, 3], 2)
+        multiply_energy(2)
+        quantize_windows()
+        add_reg(2)
+        reciprocals(0, 1)
+        interleave_target(0, 0, 0, on_vector)
+        energy_unit(3)
+        interleave_target(0, 0, 1, on_vector)
+        sort_words(4, on_scalar)
+        sort_words(5, on_scalar)
+        energy_unit(4)
+        quantize_target(0, 0)
+        energy_unit(5)
+        inverse_root(1)
+        multiply_energy(6)
+
+        turn_windows([4, 5], 2)
+        add_reg(6)
+        multiply_energy(7)
+        quantize_windows()
+        add_reg(7)
+        interleave_target(1, 0, 0, on_vector)
+        sort_words(6, on_scalar)
+        sort_words(7, on_scalar)
+        interleave_target(1, 0, 1, on_scalar)
+        energy_unit(8)
+        energy_unit(9)
+        quantize_target(1, 0)
+        multiply_energy(10)
+
+        turn_windows([6, 7], 2)
+        add_reg(10)
+        multiply_energy(11)
+        quantize_windows()
+        interleave_target(2, 0, 0, on_vector)
+        interleave_target(2, 0, 1, on_scalar)
+        add_reg(11)
+        square_root_back(1)
+        reciprocals(2, 4)
+        energy_unit(12)
+        quantize_target(2, 0)
+        interleave_whole(0, 1, on_scalar)
+        for s in range(13, UNITS):
+            energy_unit(s)
+        reciprocals(4, 7)
+        interleave_whole(1, 1, on_scalar)
+        reciprocals(7, UNITS)
 
         slopes = {}
 
@@ -315,5 +368,13 @@ def tile_guided_filter_windows_s10_kernel(tc, win, e_words, e_scales, c_words, c
             else:
                 for columns in (slice(0, 256), slice(256, 384), slice(384, 512)):
                     multiply_target(i, columns)
+            if i == 0:
+                quantize_target(0, 1)
+            if i == 2:
+                interleave_target(2, 1, 0, on_vector)
+            if i == 3:
+                quantize_target(1, 1)
             if i == 4:
+                interleave_target(2, 1, 1, on_vector)
+            if i == 5:
                 quantize_target(2, 1)

from contextlib import ExitStack

import concourse.mybir as mybir
from concourse.masks import make_identity

M, K, N = 1024, 1536, 1024
FLOPS = 3 * 2 * M * K * N

F32 = mybir.dt.float32
BF16 = mybir.dt.bfloat16
I32 = mybir.dt.int32
U32 = mybir.dt.uint32
U8 = mybir.dt.uint8
FP8X4 = mybir.dt.float8_e4m3fn_x4
FP4X4 = mybir.dt.float4_e2m1fn_x4
ACT = mybir.ActivationFunctionType
ALU = mybir.AluOpType

P = 128
PACK = 4
K_PASS = P * PACK
PASSES = K // K_PASS
TILES = M // P
HALF = 512
HALVES = N // HALF
UNITS = TILES * HALVES
BANKS = 8
RUN_BANKS = 3
GAIN_BUFS = 4


def tile_guided_filter_windows_s10_kernel(tc, win, e_words, e_scales, c_words, c_scales, target, guide, reg, out):
    nc = tc.nc
    with ExitStack() as ctx:
        keep = ctx.enter_context(tc.tile_pool(name="keep", bufs=1))
        work = ctx.enter_context(tc.tile_pool(name="work", bufs=1))
        psum = ctx.enter_context(tc.psum_pool(name="psum", bufs=1))
        ctx.enter_context(tc.manual_schedule())

        def kept(name, shape, dtype):
            return keep.tile(shape, dtype, name=name, align_bytes=64)

        free_banks = list(range(BANKS))

        def take_bank():
            index = free_banks.pop(0)
            return index, psum.tile([P, HALF], F32, name="bank%d" % index)

        e_planes = [kept("e_plane%d" % h, [P, PASSES, HALF], U8) for h in range(HALVES)]
        c_plane = kept("c_plane", [P, PASSES, N], U8)
        warm_values = kept("warm_values", [P, K_PASS], BF16)
        warm_codes = kept("warm_codes", [P, P], U32)
        warm_plane = kept("warm_plane", [P, P], U8)
        nc.gpsimd.memset(warm_values[:].bitcast(I32), 0x3F803F80)
        nc.vector.quantize_mx(out=warm_codes[:].bitcast(FP8X4), scales=warm_plane[:], in_=warm_values[:])
        for plane in e_planes + [c_plane]:
            nc.vector.memset(plane[:].bitcast(I32), 0)
        identity = kept("identity", [P, P], F32)
        make_identity(nc, identity[:])
        warm_out = kept("warm_out", [P, 8], F32)
        nc.scalar.activation(out=warm_out[:], in_=warm_values[:, 0:8], func=ACT.Abs_reciprocal_sqrt)

        win_words = {}

        def load_win(first, count):
            raw = kept("win_raw%d" % first, [P, count, K], BF16)
            nc.sync.dma_start(out=raw[:], in_=win[first * P : (first + count) * P, :].rearrange("(t p) k -> p t k", p=P))
            for t in range(count):
                win_words[first + t] = raw[:, t, :].bitcast(F32)

        def cols(h):
            return slice(h * HALF, (h + 1) * HALF)

        def load_plane(plane, scales, columns):
            rows = scales.rearrange("g (q r) n -> r q g n", r=4)
            for r in range(4):
                nc.sync.dma_start(out=plane[r:P:32, :, :].bitcast(I32), in_=rows[r, :, :, columns].bitcast(I32))

        def load_words(name, words, width):
            codes = kept(name, [P, PASSES, width], U8)
            nc.sync.dma_start(out=codes[:].bitcast(I32), in_=words.bitcast(I32))
            return codes

        target_raw = {}

        def load_target(g, h):
            raw = kept("target_raw%d_%d" % (g, h), [P, PACK, HALF], BF16)
            nc.sync.dma_start(out=raw[:], in_=target[g * K_PASS : (g + 1) * K_PASS, cols(h)].rearrange("(p j) n -> p j n", j=PACK))
            target_raw[(g, h)] = raw

        guide_rows = {}

        def load_guide(first):
            raw = kept("guide%d" % first, [P, 2, N], BF16)
            nc.sync.dma_start(out=raw[:], in_=guide[first * P : (first + 2) * P, :].rearrange("(t p) n -> p t n", p=P))
            for t in range(2):
                guide_rows[first + t] = raw[:, t, :]

        e_rows = e_words.rearrange("g p b -> p g b")
        c_rows = c_words.rearrange("g p n t -> p g (n t)")
        load_win(0, 1)
        reg_rows = kept("reg_rows", [P, N // P], BF16)
        nc.sync.dma_start(out=reg_rows[:], in_=reg.rearrange("(p c) -> p c", p=P))
        load_win(1, 1)
        load_plane(e_planes[0], e_scales, cols(0))
        e_codes = [load_words("e_codes0", e_rows[:, :, 0 : 2 * HALF], 2 * HALF)]
        load_win(2, 1)
        load_win(3, 1)
        load_plane(e_planes[1], e_scales, cols(1))
        e_codes.append(load_words("e_codes1", e_rows[:, :, 2 * HALF : 4 * HALF], 2 * HALF))
        load_target(0, 0)
        load_win(4, 1)
        load_win(5, 1)
        load_target(1, 0)
        load_win(6, 1)
        load_win(7, 1)
        load_target(2, 0)
        load_target(0, 1)
        load_plane(c_plane, c_scales, slice(0, N))
        c_codes = [load_words("c_codes0", c_rows[:, :, 0 : 4 * HALF], 4 * HALF)]
        load_guide(0)
        load_target(1, 1)
        load_guide(2)
        load_target(2, 1)
        load_guide(4)
        load_guide(6)
        c_codes.append(load_words("c_codes1", c_rows[:, :, 4 * HALF : 8 * HALF], 4 * HALF))

        win_grouped = []
        win_mx = {}

        sorted_words = {}

        def sort_words(tile, copy):
            ordered = work.tile([P, K // 2], F32, name="win_sorted", bufs=2, align_bytes=64)
            copy(
                out=ordered[:].rearrange("m (g u c i) -> m g c u i", g=PASSES, u=2, i=4),
                in_=win_words[tile].rearrange("m (g c i u) -> m g c u i", g=PASSES, u=2, i=4),
            )
            sorted_words[tile] = ordered

        def words_of(tile, g, u):
            if tile in sorted_words:
                return sorted_words[tile][:, (2 * g + u) * P : (2 * g + u + 1) * P]
            return win_words[tile][:, 2 * P * g + u : 2 * P * (g + 1) : 2]

        def turn_windows(tiles, per_bank):
            slabs = [(tile, g) for tile in tiles for g in range(PASSES)]
            held = []
            for first in range(0, len(slabs), per_bank):
                index, bank = take_bank()
                together = slabs[first : first + per_bank]
                for s, (tile, g) in enumerate(together):
                    for u in range(2):
                        col = (2 * s + u) * P
                        nc.tensor.transpose(bank[:, col : col + P], words_of(tile, g, u), identity[:])
                held.append((together, index, bank))
            for together, index, bank in held:
                count = len(together)
                grouped = work.tile([P, count * K_PASS], BF16, name="win_grouped", bufs=RUN_BANKS, align_bytes=64)
                nc.scalar.copy(
                    out=grouped[:].bitcast(F32).rearrange("p (s m u) -> p s m u", s=count, u=2),
                    in_=bank[:, 0 : count * 2 * P].rearrange("p (s u m) -> p s m u", s=count, u=2),
                )
                free_banks.append(index)
                win_grouped.append((together, grouped))

        def quantize_windows():
            for together, grouped in win_grouped:
                count = len(together)
                codes = kept("win_codes%d_%d" % together[0], [P, count * P], U32)
                plane = kept("win_plane%d_%d" % together[0], [P, count * P], U8)
                nc.vector.quantize_mx(out=codes[:].bitcast(FP8X4), scales=plane[:], in_=grouped[:])
                for s, slab in enumerate(together):
                    win_mx[slab] = (codes[:, s * P : (s + 1) * P], plane[:, s * P : (s + 1) * P])
            win_grouped.clear()

        def product(tile, operands, columns=slice(0, HALF)):
            index, bank = take_bank()
            sums = bank[:, 0 : columns.stop - columns.start]
            for g in range(PASSES):
                codes, plane = win_mx[(tile, g)]
                rhs, rhs_scale = operands[g]
                nc.tensor.matmul_mx(
                    out=sums, lhsT=codes.bitcast(FP8X4), lhsT_scale=plane, rhs=rhs[:, columns], rhs_scale=rhs_scale[:, columns],
                    start=(g == 0), stop=(g == PASSES - 1),
                )
            return index, sums

        e_operands = [[(e_codes[h][:, g, :].bitcast(FP4X4), e_planes[h][:, g, :]) for g in range(PASSES)] for h in range(HALVES)]
        c_operands = [[(c_codes[h][:, g, :].bitcast(FP8X4), c_plane[:, g, cols(h)]) for g in range(PASSES)] for h in range(HALVES)]
        t_operands = [[None] * PASSES for h in range(HALVES)]
        target_grouped = {}

        def interleave_target(g, h, part, copy):
            if (g, h) not in target_grouped:
                target_grouped[(g, h)] = work.tile([P, HALF, PACK], BF16, name="target_grouped", bufs=3, align_bytes=64)
            columns = slice(part * HALF // 2, (part + 1) * HALF // 2)
            copy(
                out=target_grouped[(g, h)][:, columns, :].rearrange("p (c i) j -> p c j i", i=4),
                in_=target_raw[(g, h)][:, :, columns].rearrange("p j (c i) -> p c j i", i=4),
            )

        def quantize_target(g, h):
            codes = kept("target_codes%d_%d" % (g, h), [P, HALF], U32)
            plane = kept("target_plane%d_%d" % (g, h), [P, HALF], U8)
            nc.vector.quantize_mx(out=codes[:].bitcast(FP8X4), scales=plane[:], in_=target_grouped[(g, h)][:].rearrange("p n j -> p (n j)"))
            t_operands[h][g] = (codes[:].bitcast(FP8X4), plane[:])

        reg_all = kept("reg_all", [P, N], BF16)

        def spread_reg():
            index, bank = take_bank()
            words = reg_rows[:].bitcast(F32)
            for c in range(4):
                nc.tensor.transpose(bank[:, c * P : (c + 1) * P], words[:, c : c + 1].to_broadcast([P, P]), identity[:])
            nc.vector.tensor_copy(
                out=reg_all[:].bitcast(F32).rearrange("q (p c) -> q p c", c=4),
                in_=bank[:].rearrange("q (c p) -> q p c", c=4),
            )
            free_banks.append(index)

        variance = {}
        divisor = {}

        energy_order = [(0, 0), (1, 0), (0, 1), (1, 1)] + [divmod(s, HALVES) for s in range(4, UNITS)]

        def multiply_energy(s):
            tile, h = energy_order[s]
            variance[s] = product(tile, e_operands[h])

        def add_reg(s):
            tile, h = energy_order[s]
            index, bank = variance[s]
            d = kept("divisor%d" % s, [P, HALF], F32)
            nc.vector.tensor_tensor(out=d[:], in0=bank, in1=reg_all[:, cols(h)], op=ALU.add)
            free_banks.append(index)
            divisor[(h, tile)] = d

        order = [(h, tile) for h in range(HALVES) for tile in range(TILES)]
        roots = {}

        def inverse_root(i):
            root = work.tile([P, HALF], F32, name="root", bufs=3)
            nc.scalar.activation(out=root[:], in_=divisor[order[i]][:], func=ACT.Abs_reciprocal_sqrt)
            roots[i] = root

        def square_root_back(i):
            nc.scalar.activation(out=divisor[order[i]][:], in_=roots[i][:], func=ACT.Square)

        gains = {}

        def make_gain(i):
            h, tile = order[i]
            gain = work.tile([P, HALF], F32, name="gain", bufs=GAIN_BUFS)
            nc.gpsimd.tensor_tensor(out=gain[:], in0=divisor[order[i]][:], in1=guide_rows[tile][:, cols(h)], op=ALU.mult)
            gains[i] = gain

        def energy_unit(s):
            multiply_energy(s)
            add_reg(s)

        def reciprocals(first, last):
            inverse_root(first)
            for i in range(first, last):
                if i + 1 < last:
                    inverse_root(i + 1)
                square_root_back(i)

        def warm_tensor_engine(count):
            index, bank = take_bank()
            for step in range(count):
                nc.tensor.matmul_mx(
                    out=bank[:, 0:P], lhsT=warm_codes[:].bitcast(FP8X4), lhsT_scale=warm_plane[:],
                    rhs=warm_codes[:].bitcast(FP8X4), rhs_scale=warm_plane[:], start=(step == 0), stop=(step == count - 1),
                )
            free_banks.append(index)

        on_vector = nc.vector.tensor_copy
        on_scalar = nc.scalar.copy
        warm_tensor_engine(12)
        def interleave_whole(g, h, copy):
            for part in range(2):
                interleave_target(g, h, part, copy)

        turn_windows([0, 1], 2)
        quantize_windows()
        spread_reg()
        energy_unit(0)
        sort_words(2, on_scalar)
        energy_unit(1)

        turn_windows([2, 3], 2)
        multiply_energy(2)
        quantize_windows()
        add_reg(2)
        reciprocals(0, 1)
        interleave_target(0, 0, 0, on_vector)
        energy_unit(3)
        interleave_target(0, 0, 1, on_vector)
        sort_words(4, on_scalar)
        sort_words(5, on_scalar)
        energy_unit(4)
        quantize_target(0, 0)
        energy_unit(5)
        inverse_root(1)
        multiply_energy(6)

        turn_windows([4, 5], 2)
        add_reg(6)
        multiply_energy(7)
        quantize_windows()
        add_reg(7)
        interleave_target(1, 0, 0, on_vector)
        sort_words(6, on_scalar)
        sort_words(7, on_scalar)
        interleave_target(1, 0, 1, on_scalar)
        energy_unit(8)
        energy_unit(9)
        quantize_target(1, 0)
        multiply_energy(10)

        turn_windows([6, 7], 2)
        add_reg(10)
        multiply_energy(11)
        quantize_windows()
        interleave_target(2, 0, 0, on_vector)
        interleave_target(2, 0, 1, on_scalar)
        add_reg(11)
        square_root_back(1)
        reciprocals(2, 4)
        energy_unit(12)
        quantize_target(2, 0)
        interleave_whole(0, 1, on_scalar)
        for s in range(13, UNITS):
            energy_unit(s)
        reciprocals(4, 7)
        interleave_whole(1, 1, on_scalar)
        reciprocals(7, UNITS)

        slopes = {}

        def multiply_cross(i):
            h, tile = order[i]
            index, bank = product(tile, c_operands[h])
            part = work.tile([P, HALF], F32, name="part", bufs=3)
            nc.vector.tensor_tensor(out=part[:], in0=bank, in1=gains[i][:], op=ALU.mult)
            free_banks.append(index)
            slopes[i] = part
            if i + GAIN_BUFS < UNITS:
                make_gain(i + GAIN_BUFS)

        def multiply_target(i, columns):
            h, tile = order[i]
            index, bank = product(tile, t_operands[h], columns)
            result = work.tile([P, columns.stop - columns.start], F32, name="result", bufs=4)
            nc.vector.tensor_tensor(out=result[:], in0=bank, in1=slopes[i][:, columns], op=ALU.add)
            free_banks.append(index)
            nc.sync.dma_start(out=out[tile * P : (tile + 1) * P, cols(h)][:, columns], in_=result[:])

        for i in range(GAIN_BUFS):
            make_gain(i)
        multiply_cross(0)
        for i in range(UNITS):
            if i + 1 < UNITS:
                multiply_cross(i + 1)
                multiply_target(i, slice(0, HALF))
            else:
                for columns in (slice(0, 256), slice(256, 384), slice(384, 512)):
                    multiply_target(i, columns)
            if i == 0:
                quantize_target(0, 1)
            if i == 2:
                interleave_target(2, 1, 0, on_vector)
            if i == 3:
                quantize_target(1, 1)
            if i == 4:
                interleave_target(2, 1, 1, on_vector)
            if i == 5:
                quantize_target(2, 1)
